import numpy as np
import ml_dtypes


def mxq(x, axis, fmt="e4m3"):
    dtype, down = {"e4m3": (ml_dtypes.float8_e4m3fn, 7), "e5m2": (ml_dtypes.float8_e5m2, 14)}[fmt]
    v = np.moveaxis(np.asarray(x, np.float32).astype(ml_dtypes.bfloat16).astype(np.float64), axis, -1)
    blocks = v.reshape(v.shape[:-1] + (-1, 32))
    amax = np.abs(blocks).max(-1, keepdims=True)
    byte = np.maximum(np.where(amax > 0, np.frexp(amax)[1] - 1 + 127, 0) - down, 1)
    scale = np.exp2(byte - 127.0)
    codes = (blocks / scale).astype(np.float32).astype(dtype).astype(np.float64)
    return np.moveaxis((codes * scale).reshape(v.shape), -1, axis)


WIDE = False


def mx_kscale(k):
    if not WIDE:
        return np.ones(k)
    levels = np.array([10, -10, 5, -5, 0])
    if k % 512:
        return np.exp2(np.random.permutation(np.resize(levels, k // 32))).repeat(32)
    a = np.empty((k // 512, 16))
    for p in range(k // 512):
        a[p, :8] = np.random.permutation(np.resize(levels, 8))
        for g in range(8):
            far = levels[np.abs(levels - a[p, g]) >= 10]
            a[p, g + 8] = far[np.random.randint(len(far))]
    return np.exp2(a.ravel()).repeat(32)


def f64(x):
    return np.asarray(x).astype(np.float64)


def striped(idx):
    return np.tile(idx.reshape(-1, 16).T, (8, 1)).astype(np.uint16)


def unstriped(offs):
    return offs[:16].T.reshape(-1).astype(np.int64)


E2M1 = np.array([0.0, 0.5, 1.0, 1.5, 2.0, 3.0, 4.0, 6.0, -0.0, -0.5, -1.0, -1.5, -2.0, -3.0, -4.0, -6.0])


def pack_weight(w, fmt):
    k, n = w.shape
    w = f64(np.asarray(w, np.float32).astype(ml_dtypes.bfloat16)).reshape(k // 32, 32, n)
    amax = np.abs(w).max(1)
    if fmt == "e4m3":
        byte = np.frexp(amax)[1] - 1 + 127 - 7
    else:
        mant, ex = np.frexp(amax / 6.0)
        byte = np.where(mant > 0.5, ex, ex - 1) + 127
    byte = np.clip(np.where(amax > 0, byte, 1), 1, 254)
    scaled = (w * np.exp2(127.0 - byte)[:, None, :]).reshape(k, n).astype(np.float32)
    by_word = np.ascontiguousarray(scaled.reshape(k // 512, 128, 4, n).transpose(0, 1, 3, 2))
    if fmt == "e4m3":
        words = by_word.astype(ml_dtypes.float8_e4m3fn).view(np.uint8)
    else:
        c = by_word.astype(ml_dtypes.float4_e2m1fn).view(np.uint8) & 0xF
        words = (c[..., 0::2] | (c[..., 1::2] << 4)).reshape(k // 512, 128, 2 * n)
    return np.ascontiguousarray(words), np.ascontiguousarray(byte.astype(np.uint8).reshape(k // 512, 16, n))


def unpack_weight(words, scales, fmt):
    g, _, n = scales.shape
    words = np.ascontiguousarray(words).reshape(g, 128, n, -1)
    if fmt == "e4m3":
        vals = words.view(ml_dtypes.float8_e4m3fn).astype(np.float64)
    else:
        nib = np.empty((g, 128, n, 4), np.uint8)
        nib[..., 0::2] = words & 0xF
        nib[..., 1::2] = words >> 4
        vals = E2M1[nib]
    vals = vals * np.repeat(np.exp2(scales.astype(np.float64) - 127.0), 8, axis=1)[..., None]
    return vals.transpose(0, 1, 3, 2).reshape(g * 512, n)


def gelu(v):
    return 0.5 * v * (1.0 + np.tanh(np.sqrt(2.0 / np.pi) * (v + 0.044715 * v**3)))


K, K2, T, S, H, N = 1024, 512, 4096, 1024, 1024, 384

def setup_inputs():
    n = np.random.standard_normal
    s = mx_kscale(K)[:, None]
    s2 = mx_kscale(K2)[:, None]
    u = mx_kscale(H)[:, None]
    d = {}
    d["tab_words"], d["tab_scales"] = pack_weight(n((K, T)) * s, "e4m3")
    d["offs"] = striped(np.random.permutation(T)[:S])
    d["xs_words"], d["xs_scales"] = pack_weight(n((K2, S)) * s2, "e4m3")
    d["w1"] = (1.2 * n((K, H)) / s / K ** 0.5).astype(np.float32)
    d["wx_words"], d["wx_scales"] = pack_weight(1.2 * n((K2, H)) / s2 / K2 ** 0.5, "e2m1")
    d["b1"] = (0.6 * n(H)).astype(np.float32)
    d["gain"] = (np.exp(0.3 * n(H)) * u[:, 0]).astype(np.float32)
    d["w2"] = (0.9 * n((H, N)) / u / H ** 0.5).astype(np.float32)
    d["w3_words"], d["w3_scales"] = pack_weight(n((H, N)) / u / H ** 0.5, "e4m3")
    return d

def reference(tab_words, tab_scales, offs, xs_words, xs_scales, w1, wx_words, wx_scales,
              b1, gain, w2, w3_words, w3_scales):
    v = unpack_weight(tab_words, tab_scales, "e4m3")[:, unstriped(offs)]
    xs = unpack_weight(xs_words, xs_scales, "e4m3")
    wx = unpack_weight(wx_words, wx_scales, "e2m1")
    w3 = unpack_weight(w3_words, w3_scales, "e4m3")
    both = mxq(f64(w1), 0, "e4m3").T @ v + wx.T @ xs
    h = f64(gain)[:, None] * np.log(1.0 + np.exp(both + f64(b1)[:, None]))
    hq = mxq(h, 0, "e4m3")
    y = mxq(f64(w2), 0, "e4m3").T @ hq
    lin = w3.T @ hq
    return np.square(y) + lin

@@ -1,0 +1,325 @@
+from contextlib import ExitStack
+
+import concourse.mybir as mybir
+
+K, K2, T, S, H, N = 1024, 512, 4096, 1024, 1024, 384
+FLOPS = 2 * (K + K2) * H * S + 4 * H * N * S
+
+F32 = mybir.dt.float32
+BF16 = mybir.dt.bfloat16
+I32 = mybir.dt.int32
+U32 = mybir.dt.uint32
+U16 = mybir.dt.uint16
+U8 = mybir.dt.uint8
+FP8X4 = mybir.dt.float8_e4m3fn_x4
+FP4X4 = mybir.dt.float4_e2m1fn_x4
+ACT = mybir.ActivationFunctionType
+ALU = mybir.AluOpType
+
+P = 128
+HALF = 512
+KNEE = 16.0
+ON_VECTOR = ((1, 0, 1), (1, 1, 2), (1, 0, 3))
+GROUPS = ((128, 128), (256,), (256,), (256,))
+
+
+def tile_list_trap_map_features_kernel(
+    tc, tab_words, tab_scales, offs, xs_words, xs_scales, w1, wx_words, wx_scales,
+    b1, gain, w2, w3_words, w3_scales, out,
+):
+    nc = tc.nc
+    with ExitStack() as ctx:
+        lists = ctx.enter_context(tc.tile_pool(name="lists", bufs=1))
+        keep = ctx.enter_context(tc.tile_pool(name="keep", bufs=1))
+        psum = ctx.enter_context(tc.psum_pool(name="psum", bufs=1))
+
+        def tile(shape, dtype, name, tag=None, bufs=1):
+            return keep.tile(shape, dtype, name=name, tag=tag or name, bufs=bufs, align_bytes=64)
+
+        offsets = lists.tile([P, S // 16], U16, name="offsets")
+        tab_w = [tile([P, T], U32, f"tab_w{a}") for a in range(2)]
+        tab_s = tile([P, T], U8, "tab_s")
+        xs_w = tile([P, S], U32, "xs_w")
+        xs_s = tile([P, S], U8, "xs_s")
+        wx_raw = tile([P, 2 * H], U8, "wx_raw")
+        wx_s_raw = tile([P, H], U8, "wx_s_raw")
+        wx_w = tile([P, 2 * H], U8, "wx_w")
+        wx_s = tile([P, H], U8, "wx_s")
+        w3_w = tile([P, 2 * N], U32, "w3_w")
+        w3_s = tile([P, N], U8, "w3_s")
+        bias = tile([P, 2, 4], F32, "bias")
+        gains = tile([P, 2, 4], F32, "gains")
+        slope = tile([P, 8], F32, "slope")
+        w2_raw = [tile([P, 4, N], F32, f"w2_raw{a}") for a in range(2)]
+
+        for plane in (tab_s, wx_s_raw, xs_s, w3_s):
+            nc.vector.memset(plane[:].bitcast(I32), 0)
+
+        def load_scale_rows(queue, plane, rows, first, r):
+            queue.dma_start(
+                plane[first + r : P : 32, :].bitcast(I32),
+                rows.rearrange("(q r) c -> r q c", r=4)[r].bitcast(I32),
+            )
+
+        w1_raw = {}
+
+        def load_w1(b, a, pieces=1):
+            w1_raw[b, a] = tile([P, 4, HALF], F32, f"w1_raw{b}{a}", tag="wide", bufs=4)
+            rows = w1[a * HALF : (a + 1) * HALF, b * HALF : (b + 1) * HALF].rearrange("(p j) c -> p j c", j=4)
+            for i in range(pieces):
+                js = slice(i * 4 // pieces, (i + 1) * 4 // pieces)
+                nc.sync.dma_start(w1_raw[b, a][:, js, :], rows[:, js, :])
+
+        def load_tab(a, h):
+            cols = slice(h * (T // 2), (h + 1) * (T // 2))
+            nc.sync.dma_start(
+                tab_w[a][:, cols].bitcast(I32),
+                tab_words[a].rearrange("p t i -> p (t i)").bitcast(I32)[:, cols],
+            )
+
+        def load_xs(c):
+            cols = slice(c * HALF, (c + 1) * HALF)
+            nc.sync.dma_start(
+                xs_w[:, cols].bitcast(I32), xs_words[0].rearrange("p c i -> p (c i)").bitcast(I32)[:, cols]
+            )
+
+        def load_w2(a):
+            nc.sync.dma_start(
+                w2_raw[a][:], w2[a * HALF : (a + 1) * HALF, :].rearrange("(p j) n -> p j n", j=4)
+            )
+
+        nc.sync.dma_start(offsets[:], offs)
+        nc.sync.dma_start(wx_raw[:].bitcast(I32), wx_words[0].bitcast(I32))
+        nc.sync.dma_start(bias[:], b1.rearrange("(b p t) -> p b t", b=2, t=4))
+        nc.sync.dma_start(gains[:], gain.rearrange("(b p t) -> p b t", b=2, t=4))
+        load_xs(0)
+        load_xs(1)
+        load_w1(0, 0, 2)
+        load_tab(0, 0)
+        for r in range(4):
+            load_scale_rows(nc.sync, tab_s, tab_scales[0], 0, r)
+        load_tab(0, 1)
+        for r in range(4):
+            load_scale_rows(nc.sync, tab_s, tab_scales[1], 4, r)
+        load_w1(0, 1)
+        for r in range(4):
+            load_scale_rows(nc.sync, wx_s_raw, wx_scales[0], 0, r)
+        load_tab(1, 0)
+        for r in range(4):
+            load_scale_rows(nc.sync, xs_s, xs_scales[0], 0, r)
+        load_tab(1, 1)
+        load_w1(1, 0)
+        load_w1(1, 1)
+        load_w2(0)
+        for q in range(4):
+            nc.sync.dma_start(
+                w3_s[32 * q : 32 * q + 8, :].bitcast(I32),
+                w3_scales[:, 4 * q : 4 * q + 4, :].bitcast(I32),
+            )
+        load_w2(1)
+        nc.sync.dma_start(
+            w3_w[:].bitcast(I32).rearrange("p (a n) -> p a n", a=2),
+            w3_words.rearrange("a p n i -> p a (n i)").bitcast(I32),
+        )
+
+        nc.vector.tensor_copy(
+            wx_w[:].rearrange("p (b t m e) -> p b m t e", b=2, t=4, e=2),
+            wx_raw[:].rearrange("p (b m t e) -> p b m t e", b=2, t=4, e=2),
+        )
+
+        w1_w, w1_s = {}, {}
+
+        def prepare_w1(b, a, on_scalar):
+            grouped = tile([P, 4 * HALF], BF16, f"w1_bf{b}{a}", tag="bf", bufs=3)
+            dst = grouped[:].rearrange("p (t m j) -> p m j t", t=4, j=4)
+            src = w1_raw[b, a][:].rearrange("p j (m t) -> p m j t", t=4)
+            if on_scalar:
+                nc.scalar.activation(dst, src, ACT.Copy)
+            else:
+                nc.vector.tensor_copy(dst, src)
+            w1_w[b, a] = tile([P, HALF], U32, f"w1_w{b}{a}")
+            w1_s[b, a] = tile([P, HALF], U8, f"w1_s{b}{a}")
+            nc.vector.quantize_mx(out=w1_w[b, a][:].bitcast(FP8X4), scales=w1_s[b, a][:], in_=grouped[:])
+
+        got_w, got_s = {}, {}
+
+        def listed(c):
+            return offsets[:, c * (HALF // 16) : (c + 1) * (HALF // 16)]
+
+        def gather_words(a, c):
+            got_w[a, c] = tile([P, HALF], U32, f"got_w{a}{c}")
+            nc.vector.tensor_copy(got_w[a, c][:], tab_w[a][:].indirect(listed(c)))
+
+        def gather_scales(c):
+            got_s[c] = tile([P, HALF], U8, f"got_s{c}")
+            nc.vector.tensor_copy(got_s[c][:], tab_s[:].indirect(listed(c)))
+
+        prepare_w1(0, 0, True)
+        for c in range(2):
+            gather_words(0, c)
+            gather_scales(c)
+        nc.vector.tensor_copy(
+            wx_s[:].rearrange("p (b t m) -> p b m t", b=2, t=4),
+            wx_s_raw[:].rearrange("p (b m t) -> p b m t", b=2, t=4),
+        )
+        prepare_w1(0, 1, True)
+        nc.vector.tensor_scalar(
+            slope[:], gains[:].rearrange("p b t -> p (b t)"), 1.0 / KNEE, None, ALU.mult
+        )
+        for c in range(2):
+            gather_words(1, c)
+
+        bank = {}
+
+        def new_bank(i, name):
+            return psum.tile([P, HALF], F32, name=name, tag=f"bank{i}")
+
+        def table_pass(b, c, t, a, start, stop):
+            m = slice(t * P, (t + 1) * P)
+            nc.tensor.matmul_mx(
+                out=bank[b, c, t][:],
+                lhsT=w1_w[b, a][:, m].bitcast(FP8X4), lhsT_scale=w1_s[b, a][:, m],
+                rhs=got_w[a, c][:].bitcast(FP8X4), rhs_scale=got_s[c][4 * a : P, :],
+                start=start, stop=stop,
+            )
+
+        def stream_pass(b, c, t, start):
+            m0 = b * HALF + t * P
+            cols = slice(c * HALF, (c + 1) * HALF)
+            nc.tensor.matmul_mx(
+                out=bank[b, c, t][:],
+                lhsT=wx_w[:, 2 * m0 : 2 * (m0 + P)].bitcast(FP4X4), lhsT_scale=wx_s[:, m0 : m0 + P],
+                rhs=xs_w[:, cols].bitcast(FP8X4), rhs_scale=xs_s[:, cols],
+                start=start, stop=False,
+            )
+
+        pre = tile([P, 8, S], F32, "pre")
+        expo = tile([P, 8, S], F32, "expo")
+
+        def leave_psum(b, c, t):
+            cols = slice(c * HALF, (c + 1) * HALF)
+            row = 4 * b + t
+            if (b, c, t) in ON_VECTOR:
+                nc.vector.tensor_scalar(pre[:, row, cols], bank[b, c, t][:], bias[:, b, t : t + 1], None, ALU.add)
+            else:
+                nc.scalar.activation(pre[:, row, cols], bank[b, c, t][:], ACT.Identity, bias=bias[:, b, t : t + 1])
+            nc.vector.tensor_scalar(expo[:, row, cols], pre[:, row, cols], KNEE, None, ALU.min)
+
+        def exp_row(row):
+            nc.scalar.activation(expo[:, row, :], expo[:, row, :], ACT.Exp)
+
+        def factor_row(row):
+            nc.vector.tensor_scalar(
+                pre[:, row, :], pre[:, row, :], KNEE, slope[:, row : row + 1], ALU.max, ALU.mult
+            )
+
+        by_c = [(c, t) for c in range(2) for t in range(4)]
+        by_t = [(c, t) for t in range(4) for c in range(2)]
+
+        for c, t in by_c:
+            bank[0, c, t] = new_bank(4 * c + t, f"s1_0{c}{t}")
+            table_pass(0, c, t, 0, True, False)
+        for c, t in by_c:
+            stream_pass(0, c, t, False)
+        for c, t in by_c:
+            table_pass(0, c, t, 1, False, True)
+            leave_psum(0, c, t)
+        prepare_w1(1, 0, False)
+        prepare_w1(1, 1, False)
+        for t in range(4):
+            exp_row(t)
+        for c, t in by_c:
+            bank[1, c, t] = new_bank(4 * c + t, f"s1_1{c}{t}")
+            stream_pass(1, c, t, True)
+        for c, t in by_t:
+            table_pass(1, c, t, 0, False, False)
+        for c, t in by_t:
+            table_pass(1, c, t, 1, False, True)
+            leave_psum(1, c, t)
+        for t in range(4):
+            exp_row(4 + t)
+
+        w2_bf = tile([P, 2 * N * 4], BF16, "w2_bf")
+        for a in range(2):
+            nc.vector.tensor_copy(
+                w2_bf[:, a * 4 * N : (a + 1) * 4 * N].rearrange("p (c i j) -> p c j i", i=4, j=4),
+                w2_raw[a][:].rearrange("p j (c i) -> p c j i", i=4),
+            )
+        w2_w = tile([P, 2 * N], U32, "w2_w")
+        w2_s = tile([P, 2 * N], U8, "w2_s")
+        for lo, hi in ((0, 512), (512, 768)):
+            nc.vector.quantize_mx(
+                out=w2_w[:, lo:hi].bitcast(FP8X4), scales=w2_s[:, lo:hi], in_=w2_bf[:, 4 * lo : 4 * hi]
+            )
+        for row in range(8):
+            factor_row(row)
+
+        def make_h(gi, g0, chunks):
+            width = sum(chunks)
+            h_w = [tile([P, width], U32, f"h_w{gi}{b}") for b in range(2)]
+            h_s = [tile([P, width], U8, f"h_s{gi}{b}") for b in range(2)]
+            c0 = 0
+            for ci, w in enumerate(chunks):
+                cols = slice(g0 + c0, g0 + c0 + w)
+                logs = tile([P, 8, w], F32, f"logs{gi}{ci}", tag="wide", bufs=4)
+                nc.scalar.activation(logs[:], expo[:, :, cols], ACT.Ln, bias=1.0)
+                h_bf = []
+                for b in range(2):
+                    h_bf.append(tile([P, 4 * w], BF16, f"h_bf{gi}{ci}{b}", tag="bf", bufs=3))
+                    nc.vector.tensor_tensor(
+                        h_bf[b][:].rearrange("p (c i t) -> p c t i", i=4, t=4),
+                        logs[:, 4 * b : 4 * b + 4, :].rearrange("p t (c i) -> p c t i", i=4),
+                        pre[:, 4 * b : 4 * b + 4, cols].rearrange("p t (c i) -> p c t i", i=4),
+                        ALU.mult,
+                    )
+                for b in range(2):
+                    nc.vector.quantize_mx(
+                        out=h_w[b][:, c0 : c0 + w].bitcast(FP8X4), scales=h_s[b][:, c0 : c0 + w], in_=h_bf[b][:]
+                    )
+                c0 += w
+            return h_w, h_s
+
+        free_banks = list(range(8))
+
+        def products(gi, width, h_w, h_s):
+            sums = []
+            for n in range(3):
+                used = [free_banks.pop(0) for k in range(2 * width // HALF)]
+                free_banks.extend(used)
+                tiles = [new_bank(i, f"s2_{gi}{n}{i}") for i in used]
+                y = tiles[0][:, :width]
+                lin = tiles[-1][:, HALF - width :]
+                for b in range(2):
+                    m = slice(b * N + n * P, b * N + (n + 1) * P)
+                    nc.tensor.matmul_mx(
+                        out=y, lhsT=w2_w[:, m].bitcast(FP8X4), lhsT_scale=w2_s[:, m],
+                        rhs=h_w[b][:].bitcast(FP8X4), rhs_scale=h_s[b][:], start=(b == 0), stop=(b == 1),
+                    )
+                for b in range(2):
+                    m = slice(b * N + n * P, b * N + (n + 1) * P)
+                    nc.tensor.matmul_mx(
+                        out=lin, lhsT=w3_w[:, m].bitcast(FP8X4),
+                        lhsT_scale=w3_s[4 * b : P, n * P : (n + 1) * P],
+                        rhs=h_w[b][:].bitcast(FP8X4), rhs_scale=h_s[b][:], start=(b == 0), stop=(b == 1),
+                    )
+                sums.append((y, lin))
+            return sums
+
+        def finish(gi, g0, width, sums):
+            for n, (y, lin) in enumerate(sums):
+                square = tile([P, width], F32, f"square{gi}{n}", tag="square", bufs=4)
+                nc.scalar.activation(square[:], y, ACT.Square)
+                result = tile([P, width], F32, f"result{gi}{n}", tag="result", bufs=4)
+                nc.vector.tensor_tensor(result[:], lin, square[:], ALU.add)
+                nc.sync.dma_start(out[n * P : (n + 1) * P, g0 : g0 + width], result[:])
+
+        g0 = 0
+        waiting = None
+        for gi, chunks in enumerate(GROUPS):
+            width = sum(chunks)
+            h_w, h_s = make_h(gi, g0, chunks)
+            if waiting:
+                finish(*waiting)
+            waiting = (gi, g0, width, products(gi, width, h_w, h_s))
+            g0 += width
+        finish(*waiting)

@@ -63,15 +63,14 @@ def tile_list_trap_map_features_kernel(
 
         w1_raw = {}
 
-        def load_w1(b, a, pieces=1):
+        def load_w1(b, a, pieces=((0, 4),)):
             w1_raw[b, a] = tile([P, 4, HALF], F32, f"w1_raw{b}{a}", tag="wide", bufs=4)
             rows = w1[a * HALF : (a + 1) * HALF, b * HALF : (b + 1) * HALF].rearrange("(p j) c -> p j c", j=4)
-            for i in range(pieces):
-                js = slice(i * 4 // pieces, (i + 1) * 4 // pieces)
-                nc.sync.dma_start(w1_raw[b, a][:, js, :], rows[:, js, :])
+            for lo, hi in pieces:
+                nc.sync.dma_start(w1_raw[b, a][:, lo:hi, :], rows[:, lo:hi, :])
 
-        def load_tab(a, h):
-            cols = slice(h * (T // 2), (h + 1) * (T // 2))
+        def load_tab(a, lo, hi):
+            cols = slice(lo, hi)
             nc.sync.dma_start(
                 tab_w[a][:, cols].bitcast(I32),
                 tab_words[a].rearrange("p t i -> p (t i)").bitcast(I32)[:, cols],
@@ -89,25 +88,27 @@ def tile_list_trap_map_features_kernel(
             )
 
         nc.sync.dma_start(offsets[:], offs)
-        nc.sync.dma_start(wx_raw[:].bitcast(I32), wx_words[0].bitcast(I32))
         nc.sync.dma_start(bias[:], b1.rearrange("(b p t) -> p b t", b=2, t=4))
         nc.sync.dma_start(gains[:], gain.rearrange("(b p t) -> p b t", b=2, t=4))
-        load_xs(0)
-        load_xs(1)
-        load_w1(0, 0, 2)
-        load_tab(0, 0)
-        for r in range(4):
-            load_scale_rows(nc.sync, tab_s, tab_scales[0], 0, r)
-        load_tab(0, 1)
-        for r in range(4):
-            load_scale_rows(nc.sync, tab_s, tab_scales[1], 4, r)
+        nc.sync.dma_start(wx_raw[:].bitcast(I32), wx_words[0].bitcast(I32))
+        load_w1(0, 0, ((0, 1), (1, 2), (2, 4)))
+        load_tab(0, 0, 512)
+        scale_rows = [(a, r) for r in range(4) for a in range(2)]
+        for a, r in scale_rows[:3]:
+            load_scale_rows(nc.sync, tab_s, tab_scales[a], 4 * a, r)
+        load_tab(0, 512, 3328)
+        for a, r in scale_rows[3:]:
+            load_scale_rows(nc.sync, tab_s, tab_scales[a], 4 * a, r)
+        load_tab(0, 3328, T)
         load_w1(0, 1)
+        load_tab(1, 0, 1536)
         for r in range(4):
             load_scale_rows(nc.sync, wx_s_raw, wx_scales[0], 0, r)
-        load_tab(1, 0)
+        load_tab(1, 1536, T)
+        load_xs(0)
         for r in range(4):
             load_scale_rows(nc.sync, xs_s, xs_scales[0], 0, r)
-        load_tab(1, 1)
+        load_xs(1)
         load_w1(1, 0)
         load_w1(1, 1)
         load_w2(0)
@@ -156,13 +157,13 @@ def tile_list_trap_map_features_kernel(
 
         prepare_w1(0, 0, True)
         for c in range(2):
-            gather_words(0, c)
             gather_scales(c)
+            gather_words(0, c)
+        prepare_w1(0, 1, True)
         nc.vector.tensor_copy(
             wx_s[:].rearrange("p (b t m) -> p b m t", b=2, t=4),
             wx_s_raw[:].rearrange("p (b m t) -> p b m t", b=2, t=4),
         )
-        prepare_w1(0, 1, True)
         nc.vector.tensor_scalar(
             slope[:], gains[:].rearrange("p b t -> p (b t)"), 1.0 / KNEE, None, ALU.mult
         )
@@ -183,14 +184,14 @@ def tile_list_trap_map_features_kernel(
                 start=start, stop=stop,
             )
 
-        def stream_pass(b, c, t, start):
+        def stream_pass(b, c, t, start, stop):
             m0 = b * HALF + t * P
             cols = slice(c * HALF, (c + 1) * HALF)
             nc.tensor.matmul_mx(
                 out=bank[b, c, t][:],
                 lhsT=wx_w[:, 2 * m0 : 2 * (m0 + P)].bitcast(FP4X4), lhsT_scale=wx_s[:, m0 : m0 + P],
                 rhs=xs_w[:, cols].bitcast(FP8X4), rhs_scale=xs_s[:, cols],
-                start=start, stop=False,
+                start=start, stop=stop,
             )
 
         pre = tile([P, 8, S], F32, "pre")
@@ -220,8 +221,7 @@ def tile_list_trap_map_features_kernel(
             bank[0, c, t] = new_bank(4 * c + t, f"s1_0{c}{t}")
             table_pass(0, c, t, 0, True, False)
         for c, t in by_c:
-            stream_pass(0, c, t, False)
-        for c, t in by_c:
+            stream_pass(0, c, t, False, False)
             table_pass(0, c, t, 1, False, True)
             leave_psum(0, c, t)
         prepare_w1(1, 0, False)
@@ -230,7 +230,7 @@ def tile_list_trap_map_features_kernel(
             exp_row(t)
         for c, t in by_c:
             bank[1, c, t] = new_bank(4 * c + t, f"s1_1{c}{t}")
-            stream_pass(1, c, t, True)
+            stream_pass(1, c, t, True, False)
         for c, t in by_t:
             table_pass(1, c, t, 0, False, False)
         for c, t in by_t:
@@ -309,7 +309,7 @@ def tile_list_trap_map_features_kernel(
             for n, (y, lin) in enumerate(sums):
                 square = tile([P, width], F32, f"square{gi}{n}", tag="square", bufs=4)
                 nc.scalar.activation(square[:], y, ACT.Square)
-                result = tile([P, width], F32, f"result{gi}{n}", tag="result", bufs=4)
+                result = tile([P, width], F32, f"result{gi}{n}")
                 nc.vector.tensor_tensor(result[:], lin, square[:], ALU.add)
                 nc.sync.dma_start(out[n * P : (n + 1) * P, g0 : g0 + width], result[:])
 

from contextlib import ExitStack

import concourse.mybir as mybir

K, K2, T, S, H, N = 1024, 512, 4096, 1024, 1024, 384
FLOPS = 2 * (K + K2) * H * S + 4 * H * N * S

F32 = mybir.dt.float32
BF16 = mybir.dt.bfloat16
I32 = mybir.dt.int32
U32 = mybir.dt.uint32
U16 = mybir.dt.uint16
U8 = mybir.dt.uint8
FP8X4 = mybir.dt.float8_e4m3fn_x4
FP4X4 = mybir.dt.float4_e2m1fn_x4
ACT = mybir.ActivationFunctionType
ALU = mybir.AluOpType

P = 128
HALF = 512
KNEE = 16.0
ON_VECTOR = ((1, 0, 1), (1, 1, 2), (1, 0, 3))
GROUPS = ((128, 128), (256,), (256,), (256,))


def tile_list_trap_map_features_kernel(
    tc, tab_words, tab_scales, offs, xs_words, xs_scales, w1, wx_words, wx_scales,
    b1, gain, w2, w3_words, w3_scales, out,
):
    nc = tc.nc
    with ExitStack() as ctx:
        lists = ctx.enter_context(tc.tile_pool(name="lists", bufs=1))
        keep = ctx.enter_context(tc.tile_pool(name="keep", bufs=1))
        psum = ctx.enter_context(tc.psum_pool(name="psum", bufs=1))

        def tile(shape, dtype, name, tag=None, bufs=1):
            return keep.tile(shape, dtype, name=name, tag=tag or name, bufs=bufs, align_bytes=64)

        offsets = lists.tile([P, S // 16], U16, name="offsets")
        tab_w = [tile([P, T], U32, f"tab_w{a}") for a in range(2)]
        tab_s = tile([P, T], U8, "tab_s")
        xs_w = tile([P, S], U32, "xs_w")
        xs_s = tile([P, S], U8, "xs_s")
        wx_raw = tile([P, 2 * H], U8, "wx_raw")
        wx_s_raw = tile([P, H], U8, "wx_s_raw")
        wx_w = tile([P, 2 * H], U8, "wx_w")
        wx_s = tile([P, H], U8, "wx_s")
        w3_w = tile([P, 2 * N], U32, "w3_w")
        w3_s = tile([P, N], U8, "w3_s")
        bias = tile([P, 2, 4], F32, "bias")
        gains = tile([P, 2, 4], F32, "gains")
        slope = tile([P, 8], F32, "slope")
        w2_raw = [tile([P, 4, N], F32, f"w2_raw{a}") for a in range(2)]

        for plane in (tab_s, wx_s_raw, xs_s, w3_s):
            nc.vector.memset(plane[:].bitcast(I32), 0)

        def load_scale_rows(queue, plane, rows, first, r):
            queue.dma_start(
                plane[first + r : P : 32, :].bitcast(I32),
                rows.rearrange("(q r) c -> r q c", r=4)[r].bitcast(I32),
            )

        w1_raw = {}

        def load_w1(b, a, pieces=((0, 4),)):
            w1_raw[b, a] = tile([P, 4, HALF], F32, f"w1_raw{b}{a}", tag="wide", bufs=4)
            rows = w1[a * HALF : (a + 1) * HALF, b * HALF : (b + 1) * HALF].rearrange("(p j) c -> p j c", j=4)
            for lo, hi in pieces:
                nc.sync.dma_start(w1_raw[b, a][:, lo:hi, :], rows[:, lo:hi, :])

        def load_tab(a, lo, hi):
            cols = slice(lo, hi)
            nc.sync.dma_start(
                tab_w[a][:, cols].bitcast(I32),
                tab_words[a].rearrange("p t i -> p (t i)").bitcast(I32)[:, cols],
            )

        def load_xs(c):
            cols = slice(c * HALF, (c + 1) * HALF)
            nc.sync.dma_start(
                xs_w[:, cols].bitcast(I32), xs_words[0].rearrange("p c i -> p (c i)").bitcast(I32)[:, cols]
            )

        def load_w2(a):
            nc.sync.dma_start(
                w2_raw[a][:], w2[a * HALF : (a + 1) * HALF, :].rearrange("(p j) n -> p j n", j=4)
            )

        nc.sync.dma_start(offsets[:], offs)
        nc.sync.dma_start(bias[:], b1.rearrange("(b p t) -> p b t", b=2, t=4))
        nc.sync.dma_start(gains[:], gain.rearrange("(b p t) -> p b t", b=2, t=4))
        nc.sync.dma_start(wx_raw[:].bitcast(I32), wx_words[0].bitcast(I32))
        load_w1(0, 0, ((0, 1), (1, 2), (2, 4)))
        load_tab(0, 0, 512)
        scale_rows = [(a, r) for r in range(4) for a in range(2)]
        for a, r in scale_rows[:3]:
            load_scale_rows(nc.sync, tab_s, tab_scales[a], 4 * a, r)
        load_tab(0, 512, 3328)
        for a, r in scale_rows[3:]:
            load_scale_rows(nc.sync, tab_s, tab_scales[a], 4 * a, r)
        load_tab(0, 3328, T)
        load_w1(0, 1)
        load_tab(1, 0, 1536)
        for r in range(4):
            load_scale_rows(nc.sync, wx_s_raw, wx_scales[0], 0, r)
        load_tab(1, 1536, T)
        load_xs(0)
        for r in range(4):
            load_scale_rows(nc.sync, xs_s, xs_scales[0], 0, r)
        load_xs(1)
        load_w1(1, 0)
        load_w1(1, 1)
        load_w2(0)
        for q in range(4):
            nc.sync.dma_start(
                w3_s[32 * q : 32 * q + 8, :].bitcast(I32),
                w3_scales[:, 4 * q : 4 * q + 4, :].bitcast(I32),
            )
        load_w2(1)
        nc.sync.dma_start(
            w3_w[:].bitcast(I32).rearrange("p (a n) -> p a n", a=2),
            w3_words.rearrange("a p n i -> p a (n i)").bitcast(I32),
        )

        nc.vector.tensor_copy(
            wx_w[:].rearrange("p (b t m e) -> p b m t e", b=2, t=4, e=2),
            wx_raw[:].rearrange("p (b m t e) -> p b m t e", b=2, t=4, e=2),
        )

        w1_w, w1_s = {}, {}

        def prepare_w1(b, a, on_scalar):
            grouped = tile([P, 4 * HALF], BF16, f"w1_bf{b}{a}", tag="bf", bufs=3)
            dst = grouped[:].rearrange("p (t m j) -> p m j t", t=4, j=4)
            src = w1_raw[b, a][:].rearrange("p j (m t) -> p m j t", t=4)
            if on_scalar:
                nc.scalar.activation(dst, src, ACT.Copy)
            else:
                nc.vector.tensor_copy(dst, src)
            w1_w[b, a] = tile([P, HALF], U32, f"w1_w{b}{a}")
            w1_s[b, a] = tile([P, HALF], U8, f"w1_s{b}{a}")
            nc.vector.quantize_mx(out=w1_w[b, a][:].bitcast(FP8X4), scales=w1_s[b, a][:], in_=grouped[:])

        got_w, got_s = {}, {}

        def listed(c):
            return offsets[:, c * (HALF // 16) : (c + 1) * (HALF // 16)]

        def gather_words(a, c):
            got_w[a, c] = tile([P, HALF], U32, f"got_w{a}{c}")
            nc.vector.tensor_copy(got_w[a, c][:], tab_w[a][:].indirect(listed(c)))

        def gather_scales(c):
            got_s[c] = tile([P, HALF], U8, f"got_s{c}")
            nc.vector.tensor_copy(got_s[c][:], tab_s[:].indirect(listed(c)))

        prepare_w1(0, 0, True)
        for c in range(2):
            gather_scales(c)
            gather_words(0, c)
        prepare_w1(0, 1, True)
        nc.vector.tensor_copy(
            wx_s[:].rearrange("p (b t m) -> p b m t", b=2, t=4),
            wx_s_raw[:].rearrange("p (b m t) -> p b m t", b=2, t=4),
        )
        nc.vector.tensor_scalar(
            slope[:], gains[:].rearrange("p b t -> p (b t)"), 1.0 / KNEE, None, ALU.mult
        )
        for c in range(2):
            gather_words(1, c)

        bank = {}

        def new_bank(i, name):
            return psum.tile([P, HALF], F32, name=name, tag=f"bank{i}")

        def table_pass(b, c, t, a, start, stop):
            m = slice(t * P, (t + 1) * P)
            nc.tensor.matmul_mx(
                out=bank[b, c, t][:],
                lhsT=w1_w[b, a][:, m].bitcast(FP8X4), lhsT_scale=w1_s[b, a][:, m],
                rhs=got_w[a, c][:].bitcast(FP8X4), rhs_scale=got_s[c][4 * a : P, :],
                start=start, stop=stop,
            )

        def stream_pass(b, c, t, start, stop):
            m0 = b * HALF + t * P
            cols = slice(c * HALF, (c + 1) * HALF)
            nc.tensor.matmul_mx(
                out=bank[b, c, t][:],
                lhsT=wx_w[:, 2 * m0 : 2 * (m0 + P)].bitcast(FP4X4), lhsT_scale=wx_s[:, m0 : m0 + P],
                rhs=xs_w[:, cols].bitcast(FP8X4), rhs_scale=xs_s[:, cols],
                start=start, stop=stop,
            )

        pre = tile([P, 8, S], F32, "pre")
        expo = tile([P, 8, S], F32, "expo")

        def leave_psum(b, c, t):
            cols = slice(c * HALF, (c + 1) * HALF)
            row = 4 * b + t
            if (b, c, t) in ON_VECTOR:
                nc.vector.tensor_scalar(pre[:, row, cols], bank[b, c, t][:], bias[:, b, t : t + 1], None, ALU.add)
            else:
                nc.scalar.activation(pre[:, row, cols], bank[b, c, t][:], ACT.Identity, bias=bias[:, b, t : t + 1])
            nc.vector.tensor_scalar(expo[:, row, cols], pre[:, row, cols], KNEE, None, ALU.min)

        def exp_row(row):
            nc.scalar.activation(expo[:, row, :], expo[:, row, :], ACT.Exp)

        def factor_row(row):
            nc.vector.tensor_scalar(
                pre[:, row, :], pre[:, row, :], KNEE, slope[:, row : row + 1], ALU.max, ALU.mult
            )

        by_c = [(c, t) for c in range(2) for t in range(4)]
        by_t = [(c, t) for t in range(4) for c in range(2)]

        for c, t in by_c:
            bank[0, c, t] = new_bank(4 * c + t, f"s1_0{c}{t}")
            table_pass(0, c, t, 0, True, False)
        for c, t in by_c:
            stream_pass(0, c, t, False, False)
            table_pass(0, c, t, 1, False, True)
            leave_psum(0, c, t)
        prepare_w1(1, 0, False)
        prepare_w1(1, 1, False)
        for t in range(4):
            exp_row(t)
        for c, t in by_c:
            bank[1, c, t] = new_bank(4 * c + t, f"s1_1{c}{t}")
            stream_pass(1, c, t, True, False)
        for c, t in by_t:
            table_pass(1, c, t, 0, False, False)
        for c, t in by_t:
            table_pass(1, c, t, 1, False, True)
            leave_psum(1, c, t)
        for t in range(4):
            exp_row(4 + t)

        w2_bf = tile([P, 2 * N * 4], BF16, "w2_bf")
        for a in range(2):
            nc.vector.tensor_copy(
                w2_bf[:, a * 4 * N : (a + 1) * 4 * N].rearrange("p (c i j) -> p c j i", i=4, j=4),
                w2_raw[a][:].rearrange("p j (c i) -> p c j i", i=4),
            )
        w2_w = tile([P, 2 * N], U32, "w2_w")
        w2_s = tile([P, 2 * N], U8, "w2_s")
        for lo, hi in ((0, 512), (512, 768)):
            nc.vector.quantize_mx(
                out=w2_w[:, lo:hi].bitcast(FP8X4), scales=w2_s[:, lo:hi], in_=w2_bf[:, 4 * lo : 4 * hi]
            )
        for row in range(8):
            factor_row(row)

        def make_h(gi, g0, chunks):
            width = sum(chunks)
            h_w = [tile([P, width], U32, f"h_w{gi}{b}") for b in range(2)]
            h_s = [tile([P, width], U8, f"h_s{gi}{b}") for b in range(2)]
            c0 = 0
            for ci, w in enumerate(chunks):
                cols = slice(g0 + c0, g0 + c0 + w)
                logs = tile([P, 8, w], F32, f"logs{gi}{ci}", tag="wide", bufs=4)
                nc.scalar.activation(logs[:], expo[:, :, cols], ACT.Ln, bias=1.0)
                h_bf = []
                for b in range(2):
                    h_bf.append(tile([P, 4 * w], BF16, f"h_bf{gi}{ci}{b}", tag="bf", bufs=3))
                    nc.vector.tensor_tensor(
                        h_bf[b][:].rearrange("p (c i t) -> p c t i", i=4, t=4),
                        logs[:, 4 * b : 4 * b + 4, :].rearrange("p t (c i) -> p c t i", i=4),
                        pre[:, 4 * b : 4 * b + 4, cols].rearrange("p t (c i) -> p c t i", i=4),
                        ALU.mult,
                    )
                for b in range(2):
                    nc.vector.quantize_mx(
                        out=h_w[b][:, c0 : c0 + w].bitcast(FP8X4), scales=h_s[b][:, c0 : c0 + w], in_=h_bf[b][:]
                    )
                c0 += w
            return h_w, h_s

        free_banks = list(range(8))

        def products(gi, width, h_w, h_s):
            sums = []
            for n in range(3):
                used = [free_banks.pop(0) for k in range(2 * width // HALF)]
                free_banks.extend(used)
                tiles = [new_bank(i, f"s2_{gi}{n}{i}") for i in used]
                y = tiles[0][:, :width]
                lin = tiles[-1][:, HALF - width :]
                for b in range(2):
                    m = slice(b * N + n * P, b * N + (n + 1) * P)
                    nc.tensor.matmul_mx(
                        out=y, lhsT=w2_w[:, m].bitcast(FP8X4), lhsT_scale=w2_s[:, m],
                        rhs=h_w[b][:].bitcast(FP8X4), rhs_scale=h_s[b][:], start=(b == 0), stop=(b == 1),
                    )
                for b in range(2):
                    m = slice(b * N + n * P, b * N + (n + 1) * P)
                    nc.tensor.matmul_mx(
                        out=lin, lhsT=w3_w[:, m].bitcast(FP8X4),
                        lhsT_scale=w3_s[4 * b : P, n * P : (n + 1) * P],
                        rhs=h_w[b][:].bitcast(FP8X4), rhs_scale=h_s[b][:], start=(b == 0), stop=(b == 1),
                    )
                sums.append((y, lin))
            return sums

        def finish(gi, g0, width, sums):
            for n, (y, lin) in enumerate(sums):
                square = tile([P, width], F32, f"square{gi}{n}", tag="square", bufs=4)
                nc.scalar.activation(square[:], y, ACT.Square)
                result = tile([P, width], F32, f"result{gi}{n}")
                nc.vector.tensor_tensor(result[:], lin, square[:], ALU.add)
                nc.sync.dma_start(out[n * P : (n + 1) * P, g0 : g0 + width], result[:])

        g0 = 0
        waiting = None
        for gi, chunks in enumerate(GROUPS):
            width = sum(chunks)
            h_w, h_s = make_h(gi, g0, chunks)
            if waiting:
                finish(*waiting)
            waiting = (gi, g0, width, products(gi, width, h_w, h_s))
            g0 += width
        finish(*waiting)
